import numpy as np
import ml_dtypes

BF16 = ml_dtypes.bfloat16


def bf(x):
    return np.asarray(x, np.float32).astype(BF16)


def f32(x):
    return np.asarray(x, np.float32)


def f64(x):
    return np.asarray(x).astype(np.float64)


def striped(idx):
    return np.tile(idx.reshape(-1, 16).T, (8, 1))


S, K, H, M, N, E, Q = 512, 128, 256, 128, 128, 2, 64


def gelu_tanh(v):
    return 0.5 * v * (1.0 + np.tanh(np.sqrt(2.0 / np.pi) * (v + 0.044715 * v**3)))


def setup_inputs():
    return {"base": bf(np.random.standard_normal((M, S))), "x": bf(np.random.standard_normal((K, N))), "w": bf(np.random.standard_normal((E, K, H)) / np.sqrt(K)), "b": f32(0.5 * np.random.standard_normal((H, E))), "w2": bf(1.5 * np.random.standard_normal((E, H, M)) / np.sqrt(H)), "offs": striped(np.random.permutation(S)[:N])}


def reference(base, x, w, b, w2, offs):
    idx = offs[:16].T.reshape(-1)
    z = f64(base).copy()
    for e in range(E):
        t = f64(w)[e].T @ f64(x)[:, e * Q : (e + 1) * Q] + f64(b)[:, e : e + 1]
        t = gelu_tanh(t)
        z[:, idx[e * Q : (e + 1) * Q]] += f64(w2)[e].T @ t
    return z

@@ -1,0 +1,65 @@
+import concourse.mybir as mybir
+from concourse.masks import make_identity
+
+BF16, F32, U16 = mybir.dt.bfloat16, mybir.dt.float32, mybir.dt.uint16
+GELU = mybir.ActivationFunctionType.Gelu_apprx_tanh
+
+P = 128
+S = 512
+E = 2
+Q = 64
+HALVES = 2
+LIST_COLUMNS = Q // 16
+
+FLOPS = 2 * (E * Q) * (P * HALVES * P) * 2
+
+
+def tile_rows_ffnback_gelu_kernel(tc, base, x, w, b, w2, offs, out):
+    nc = tc.nc
+    with (
+        tc.tile_pool(name="held", bufs=1) as held,
+        tc.psum_pool(name="psum", bufs=1) as psum,
+    ):
+        x_sb = held.tile([P, E * Q], BF16, name="x_sb")
+        w_sb = held.tile([P, E, HALVES * P], BF16, name="w_sb")
+        b_sb = held.tile([P, HALVES * E], F32, name="b_sb")
+        base_sb = held.tile([P, S], BF16, name="base_sb")
+        offsets = held.tile([P, E * LIST_COLUMNS], U16, name="offsets")
+        w2_sb = held.tile([P, E, HALVES * P], BF16, name="w2_sb")
+
+        nc.sync.dma_start(x_sb[:], x)
+        nc.sync.dma_start(w_sb[:], w.rearrange("e k h -> k e h"))
+        nc.sync.dma_start(b_sb[:], b.rearrange("(p a) e -> p (a e)", a=HALVES))
+        nc.sync.dma_start(base_sb[:], base)
+        nc.sync.dma_start(offsets[:], offs)
+        nc.sync.dma_start(w2_sb[:], w2.rearrange("e (p a) m -> p e (a m)", a=HALVES))
+
+        identity = held.tile([P, P], BF16, name="identity")
+        make_identity(nc, identity[:])
+
+        hidden = {}
+        for e in range(E):
+            for a in range(HALVES):
+                product = psum.tile([P, Q], F32, name=f"product_{e}_{a}")
+                nc.tensor.matmul(
+                    product[:], w_sb[:, e, a::HALVES], x_sb[:, e * Q : (e + 1) * Q], start=True, stop=True
+                )
+                h = held.tile([P, Q], BF16, name=f"h_{e}_{a}")
+                column = a * E + e
+                nc.scalar.activation(h[:], product[:], GELU, bias=b_sb[:, column : column + 1])
+                hidden[e, a] = h
+
+        window = psum.tile([P, S], F32, name="window")
+        nc.tensor.matmul(window[:], identity[:], base_sb[:], start=True, stop=False)
+
+        for e in range(E):
+            places = window[:].indirect(offsets[:, e * LIST_COLUMNS : (e + 1) * LIST_COLUMNS])
+            for a in range(HALVES):
+                last = e == E - 1 and a == HALVES - 1
+                nc.tensor.matmul(
+                    places, w2_sb[:, e, a * P : (a + 1) * P], hidden[e, a][:], start=False, stop=last
+                )
+
+        z = held.tile([P, S], F32, name="z")
+        nc.vector.tensor_copy(z[:], window[:])
+        nc.sync.dma_start(out, z[:])

@@ -10,6 +10,7 @@ E = 2
 Q = 64
 HALVES = 2
 LIST_COLUMNS = Q // 16
+WARM_UPS = 14
 
 FLOPS = 2 * (E * Q) * (P * HALVES * P) * 2
 
@@ -33,6 +34,16 @@ def tile_rows_ffnback_gelu_kernel(tc, base, x, w, b, w2, offs, out):
         nc.sync.dma_start(base_sb[:], base)
         nc.sync.dma_start(offsets[:], offs)
         nc.sync.dma_start(w2_sb[:], w2.rearrange("e (p a) m -> p e (a m)", a=HALVES))
+
+        zeros = held.tile([P, P], BF16, name="zeros")
+        nc.gpsimd.memset(zeros[:], 0.0)
+
+        table_call = held.tile([P, 1], BF16, name="table_call")
+        nc.scalar.activation(table_call[:], zeros[:, 0:1], GELU)
+
+        warm = psum.tile([P, P], F32, name="warm")
+        for turn in range(WARM_UPS):
+            nc.tensor.matmul(warm[:], zeros[:], zeros[:], start=True, stop=True)
 
         identity = held.tile([P, P], BF16, name="identity")
         make_identity(nc, identity[:])

@@ -72,5 +72,7 @@ def tile_rows_ffnback_gelu_kernel(tc, base, x, w, b, w2, offs, out):
                 )
 
         z = held.tile([P, S], F32, name="z")
-        nc.vector.tensor_copy(z[:], window[:])
-        nc.sync.dma_start(out, z[:])
+        for part in range(2):
+            columns = slice(part * S // 2, (part + 1) * S // 2)
+            nc.vector.tensor_copy(z[:, columns], window[:, columns])
+            nc.sync.dma_start(out[:, columns], z[:, columns])

import concourse.mybir as mybir
from concourse.masks import make_identity

BF16, F32, U16 = mybir.dt.bfloat16, mybir.dt.float32, mybir.dt.uint16
GELU = mybir.ActivationFunctionType.Gelu_apprx_tanh

P = 128
S = 512
E = 2
Q = 64
HALVES = 2
LIST_COLUMNS = Q // 16
WARM_UPS = 14

FLOPS = 2 * (E * Q) * (P * HALVES * P) * 2


def tile_rows_ffnback_gelu_kernel(tc, base, x, w, b, w2, offs, out):
    nc = tc.nc
    with (
        tc.tile_pool(name="held", bufs=1) as held,
        tc.psum_pool(name="psum", bufs=1) as psum,
    ):
        x_sb = held.tile([P, E * Q], BF16, name="x_sb")
        w_sb = held.tile([P, E, HALVES * P], BF16, name="w_sb")
        b_sb = held.tile([P, HALVES * E], F32, name="b_sb")
        base_sb = held.tile([P, S], BF16, name="base_sb")
        offsets = held.tile([P, E * LIST_COLUMNS], U16, name="offsets")
        w2_sb = held.tile([P, E, HALVES * P], BF16, name="w2_sb")

        nc.sync.dma_start(x_sb[:], x)
        nc.sync.dma_start(w_sb[:], w.rearrange("e k h -> k e h"))
        nc.sync.dma_start(b_sb[:], b.rearrange("(p a) e -> p (a e)", a=HALVES))
        nc.sync.dma_start(base_sb[:], base)
        nc.sync.dma_start(offsets[:], offs)
        nc.sync.dma_start(w2_sb[:], w2.rearrange("e (p a) m -> p e (a m)", a=HALVES))

        zeros = held.tile([P, P], BF16, name="zeros")
        nc.gpsimd.memset(zeros[:], 0.0)

        table_call = held.tile([P, 1], BF16, name="table_call")
        nc.scalar.activation(table_call[:], zeros[:, 0:1], GELU)

        warm = psum.tile([P, P], F32, name="warm")
        for turn in range(WARM_UPS):
            nc.tensor.matmul(warm[:], zeros[:], zeros[:], start=True, stop=True)

        identity = held.tile([P, P], BF16, name="identity")
        make_identity(nc, identity[:])

        hidden = {}
        for e in range(E):
            for a in range(HALVES):
                product = psum.tile([P, Q], F32, name=f"product_{e}_{a}")
                nc.tensor.matmul(
                    product[:], w_sb[:, e, a::HALVES], x_sb[:, e * Q : (e + 1) * Q], start=True, stop=True
                )
                h = held.tile([P, Q], BF16, name=f"h_{e}_{a}")
                column = a * E + e
                nc.scalar.activation(h[:], product[:], GELU, bias=b_sb[:, column : column + 1])
                hidden[e, a] = h

        window = psum.tile([P, S], F32, name="window")
        nc.tensor.matmul(window[:], identity[:], base_sb[:], start=True, stop=False)

        for e in range(E):
            places = window[:].indirect(offsets[:, e * LIST_COLUMNS : (e + 1) * LIST_COLUMNS])
            for a in range(HALVES):
                last = e == E - 1 and a == HALVES - 1
                nc.tensor.matmul(
                    places, w2_sb[:, e, a * P : (a + 1) * P], hidden[e, a][:], start=False, stop=last
                )

        z = held.tile([P, S], F32, name="z")
        for part in range(2):
            columns = slice(part * S // 2, (part + 1) * S // 2)
            nc.vector.tensor_copy(z[:, columns], window[:, columns])
            nc.sync.dma_start(out[:, columns], z[:, columns])
